import numpy as np
import ml_dtypes

BF16 = ml_dtypes.bfloat16


def bf(x):
    return np.asarray(x, np.float32).astype(BF16)


def f32(x):
    return np.asarray(x, np.float32)


def f64(x):
    return np.asarray(x).astype(np.float64)


def striped(idx):
    return np.tile(idx.reshape(-1, 16).T, (8, 1))


def rows(idx, k):
    return np.tile(idx, (k, 1))


def look(tab, idx):
    return np.take_along_axis(f64(tab), rows(idx, len(tab)), axis=1)


K, S, D, V, N, M = 512, 2048, 3, 512, 1536, 128


def setup_inputs():
    return {"tab": f32(np.random.standard_normal((K, S))), "u0": f32(np.random.uniform(0.2, 1.0, (K, V))), "u1": f32(np.random.uniform(0.2, 1.0, (K, V))), "u2": f32(np.random.uniform(0.2, 1.0, (K, V))), "w": bf(np.random.standard_normal((K, M)) / np.sqrt(K)), "b": f32(0.5 * np.random.standard_normal((M, 1))), "offs": striped(np.random.permutation(S)[:N])}


def reference(tab, u0, u1, u2, w, b, offs):
    idx = offs[:16].T.reshape(-1)
    x = f64(u0) * np.minimum(np.maximum(look(tab, idx[:V]), -1.25), 1.0) + f64(u1) * np.minimum(np.maximum(look(tab, idx[1 * V:2 * V]), -1.25), 1.0) + f64(u2) * np.minimum(np.maximum(look(tab, idx[2 * V:3 * V]), -1.25), 1.0)
    return np.maximum(f64(w).T @ x + f64(b), 0.0)

@@ -1,0 +1,64 @@
+import concourse.mybir as mybir
+
+F32, BF16, U16 = mybir.dt.float32, mybir.dt.bfloat16, mybir.dt.uint16
+ALU = mybir.AluOpType
+ACT = mybir.ActivationFunctionType
+
+P = 128
+GROUP = 16
+LOW, HIGH = -1.25, 1.0
+FLOPS = 2 * 512 * 128 * 512
+
+
+def tile_lookup_clipmix_relu_kernel(tc, tab, u0, u1, u2, w, b, offs, out):
+    nc = tc.nc
+    rows, table_cols = tab.shape
+    picks = u0.shape[1]
+    features = w.shape[1]
+    blocks = rows // P
+    mixes = (u0, u1, u2)
+    pick_cols = picks // GROUP
+
+    def block_rows(array, k):
+        return array.rearrange("(p k) c -> k p c", k=blocks)[k]
+
+    with (
+        tc.tile_pool(name="held", bufs=1) as held,
+        tc.psum_pool(name="psum", bufs=1) as psum,
+    ):
+        offsets = held.tile(list(offs.shape), U16, name="offsets")
+        nc.sync.dma_start(offsets[:], offs)
+
+        tables, weights = [], []
+        layer_bf16 = held.tile([P, blocks, features], BF16, name="layer_bf16")
+        bias = held.tile([features, 1], F32, name="bias")
+        for k in range(blocks):
+            table = held.tile([P, table_cols], F32, name=f"table{k}")
+            nc.sync.dma_start(table[:], block_rows(tab, k))
+            tables.append(table)
+            if k == 0:
+                nc.sync.dma_start(layer_bf16[:], w.rearrange("(p k) m -> p k m", k=blocks))
+                nc.sync.dma_start(bias[:], b)
+            for d, mix in enumerate(mixes):
+                weight = held.tile([P, picks], F32, name=f"weight{k}_{d}")
+                nc.sync.dma_start(weight[:], block_rows(mix, k))
+                weights.append(weight)
+
+        layer = held.tile([P, blocks, features], F32, name="layer")
+        nc.scalar.copy(layer[:], layer_bf16[:])
+
+        acc = psum.tile([features, picks], F32, name="acc")
+        terms = blocks * len(mixes)
+        for k in range(blocks):
+            for d in range(len(mixes)):
+                term = k * len(mixes) + d
+                clamped = held.tile([P, picks], F32, name=f"clamped{term}")
+                looked_up = tables[k][:].indirect(offsets[:, d * pick_cols : (d + 1) * pick_cols])
+                nc.vector.tensor_scalar(clamped[:], looked_up, LOW, HIGH, ALU.max, ALU.min)
+                product = held.tile([P, picks], F32, name=f"product{term}")
+                nc.gpsimd.tensor_tensor(product[:], clamped[:], weights[term][:], ALU.mult)
+                nc.tensor.matmul(acc[:], layer[:, k, :], product[:], start=term == 0, stop=term == terms - 1)
+
+        result = held.tile([features, picks], F32, name="result")
+        nc.scalar.activation(result[:], acc[:], ACT.Relu, bias=bias[:])
+        nc.sync.dma_start(out, result[:])

@@ -7,6 +7,7 @@ ACT = mybir.ActivationFunctionType
 P = 128
 GROUP = 16
 LOW, HIGH = -1.25, 1.0
+WARM_UP = 16
 FLOPS = 2 * 512 * 128 * 512
 
 
@@ -17,7 +18,9 @@ def tile_lookup_clipmix_relu_kernel(tc, tab, u0, u1, u2, w, b, offs, out):
     features = w.shape[1]
     blocks = rows // P
     mixes = (u0, u1, u2)
-    pick_cols = picks // GROUP
+    depth = len(mixes)
+    half = picks // 2
+    left, right = slice(0, half), slice(half, picks)
 
     def block_rows(array, k):
         return array.rearrange("(p k) c -> k p c", k=blocks)[k]
@@ -27,38 +30,65 @@ def tile_lookup_clipmix_relu_kernel(tc, tab, u0, u1, u2, w, b, offs, out):
         tc.psum_pool(name="psum", bufs=1) as psum,
     ):
         offsets = held.tile(list(offs.shape), U16, name="offsets")
-        nc.sync.dma_start(offsets[:], offs)
-
-        tables, weights = [], []
+        tables = [held.tile([P, table_cols], F32, name=f"table{k}") for k in range(blocks)]
+        weights = [held.tile([P, depth, picks], F32, name=f"weights{k}") for k in range(blocks)]
         layer_bf16 = held.tile([P, blocks, features], BF16, name="layer_bf16")
         bias = held.tile([features, 1], F32, name="bias")
-        for k in range(blocks):
-            table = held.tile([P, table_cols], F32, name=f"table{k}")
-            nc.sync.dma_start(table[:], block_rows(tab, k))
-            tables.append(table)
-            if k == 0:
-                nc.sync.dma_start(layer_bf16[:], w.rearrange("(p k) m -> p k m", k=blocks))
-                nc.sync.dma_start(bias[:], b)
-            for d, mix in enumerate(mixes):
-                weight = held.tile([P, picks], F32, name=f"weight{k}_{d}")
-                nc.sync.dma_start(weight[:], block_rows(mix, k))
-                weights.append(weight)
 
-        layer = held.tile([P, blocks, features], F32, name="layer")
-        nc.scalar.copy(layer[:], layer_bf16[:])
+        nc.sync.dma_start(offsets[:], offs)
+        nc.sync.dma_start(tables[0][:], block_rows(tab, 0))
+        nc.sync.dma_start(layer_bf16[:], w.rearrange("(p k) m -> p k m", k=blocks))
+        for k in range(blocks):
+            for d in range(depth):
+                if d == depth - 1 and k + 1 < blocks:
+                    nc.sync.dma_start(tables[k + 1][:], block_rows(tab, k + 1))
+                nc.sync.dma_start(weights[k][:, d, :], block_rows(mixes[d], k))
+        nc.sync.dma_start(bias[:], b)
+
+        zeros = held.tile([P, picks], BF16, name="zeros")
+        nc.vector.memset(zeros[:], 0.0)
+        scratch = psum.tile([P, picks], F32, name="scratch")
+        for step in range(WARM_UP):
+            nc.tensor.matmul(scratch[:], zeros[:, :P], zeros[:], start=True, stop=True)
+
+        layer_f32 = held.tile([P, blocks, features], F32, name="layer_f32")
+        nc.scalar.copy(layer_f32[:], layer_bf16[:])
+
+        def clamped_look_up(dst, k, d, cols):
+            first, last = d * picks + cols.start, d * picks + cols.stop
+            window = tables[k][:].indirect(offsets[:, first // GROUP : last // GROUP])
+            nc.vector.tensor_scalar(dst, window, LOW, HIGH, ALU.max, ALU.min)
 
         acc = psum.tile([features, picks], F32, name="acc")
-        terms = blocks * len(mixes)
-        for k in range(blocks):
-            for d in range(len(mixes)):
-                term = k * len(mixes) + d
-                clamped = held.tile([P, picks], F32, name=f"clamped{term}")
-                looked_up = tables[k][:].indirect(offsets[:, d * pick_cols : (d + 1) * pick_cols])
-                nc.vector.tensor_scalar(clamped[:], looked_up, LOW, HIGH, ALU.max, ALU.min)
-                product = held.tile([P, picks], F32, name=f"product{term}")
-                nc.gpsimd.tensor_tensor(product[:], clamped[:], weights[term][:], ALU.mult)
-                nc.tensor.matmul(acc[:], layer[:, k, :], product[:], start=term == 0, stop=term == terms - 1)
+        for k in range(blocks - 1):
+            clamped = held.tile([P, depth, picks], F32, name=f"clamped{k}")
+            products = held.tile([P, depth, picks], F32, name=f"products{k}")
+            for d in range(depth):
+                clamped_look_up(clamped[:, d, :], k, d, slice(0, picks))
+                nc.gpsimd.tensor_tensor(products[:, d, :], clamped[:, d, :], weights[k][:, d, :], ALU.mult)
+                nc.tensor.matmul(acc[:], layer_f32[:, k, :], products[:, d, :], start=k == 0 and d == 0, stop=False)
+
+        k = blocks - 1
+        clamped_left = held.tile([P, depth, half], F32, name="clamped_left")
+        products_left = held.tile([P, depth, half], F32, name="products_left")
+        for d in range(depth):
+            clamped_look_up(clamped_left[:, d, :], k, d, left)
+        nc.gpsimd.tensor_tensor(products_left[:], clamped_left[:], weights[k][:, :, left], ALU.mult)
+        for d in range(depth):
+            nc.tensor.matmul(acc[:, left], layer_f32[:, k, :], products_left[:, d, :], start=False, stop=False)
+
+        clamped_right = held.tile([P, depth, half], F32, name="clamped_right")
+        products_right = held.tile([P, depth, half], F32, name="products_right")
+        pair_sum = held.tile([P, half], F32, name="pair_sum")
+        x_right = held.tile([P, half], BF16, name="x_right")
+        for d in range(depth):
+            clamped_look_up(clamped_right[:, d, :], k, d, right)
+        nc.vector.tensor_tensor(products_right[:], clamped_right[:], weights[k][:, :, right], ALU.mult)
+        nc.vector.tensor_tensor(pair_sum[:], products_right[:, 0, :], products_right[:, 1, :], ALU.add)
+        nc.vector.tensor_tensor(x_right[:], pair_sum[:], products_right[:, 2, :], ALU.add)
+        nc.tensor.matmul(acc[:, right], layer_bf16[:, k, :], x_right[:], start=False, stop=True)
 
         result = held.tile([features, picks], F32, name="result")
-        nc.scalar.activation(result[:], acc[:], ACT.Relu, bias=bias[:])
-        nc.sync.dma_start(out, result[:])
+        for cols in (left, right):
+            nc.scalar.activation(result[:, cols], acc[:, cols], ACT.Relu, bias=bias[:])
+            nc.sync.dma_start(out[:, cols], result[:, cols])

@@ -7,7 +7,6 @@ ACT = mybir.ActivationFunctionType
 P = 128
 GROUP = 16
 LOW, HIGH = -1.25, 1.0
-WARM_UP = 16
 FLOPS = 2 * 512 * 128 * 512
 
 
@@ -17,10 +16,11 @@ def tile_lookup_clipmix_relu_kernel(tc, tab, u0, u1, u2, w, b, offs, out):
     picks = u0.shape[1]
     features = w.shape[1]
     blocks = rows // P
+    last = blocks - 1
     mixes = (u0, u1, u2)
     depth = len(mixes)
     half = picks // 2
-    left, right = slice(0, half), slice(half, picks)
+    whole, left, right = slice(0, picks), slice(0, half), slice(half, picks)
 
     def block_rows(array, k):
         return array.rearrange("(p k) c -> k p c", k=blocks)[k]
@@ -31,64 +31,69 @@ def tile_lookup_clipmix_relu_kernel(tc, tab, u0, u1, u2, w, b, offs, out):
     ):
         offsets = held.tile(list(offs.shape), U16, name="offsets")
         tables = [held.tile([P, table_cols], F32, name=f"table{k}") for k in range(blocks)]
-        weights = [held.tile([P, depth, picks], F32, name=f"weights{k}") for k in range(blocks)]
+        weights = [held.tile([P, depth, picks], F32, name=f"weights{k}") for k in range(last)]
+        weights_left = held.tile([P, depth, half], F32, name="weights_left")
+        weights_right = held.tile([P, depth, half], F32, name="weights_right")
         layer_bf16 = held.tile([P, blocks, features], BF16, name="layer_bf16")
         bias = held.tile([features, 1], F32, name="bias")
 
-        nc.sync.dma_start(offsets[:], offs)
         nc.sync.dma_start(tables[0][:], block_rows(tab, 0))
+        nc.sync.dma_start(offsets[:], offs)
         nc.sync.dma_start(layer_bf16[:], w.rearrange("(p k) m -> p k m", k=blocks))
-        for k in range(blocks):
+        for k in range(last):
             for d in range(depth):
-                if d == depth - 1 and k + 1 < blocks:
+                if d == depth - 1:
                     nc.sync.dma_start(tables[k + 1][:], block_rows(tab, k + 1))
                 nc.sync.dma_start(weights[k][:, d, :], block_rows(mixes[d], k))
+        for tile, cols in ((weights_left, left), (weights_right, right)):
+            for d in range(depth):
+                nc.sync.dma_start(tile[:, d, :], block_rows(mixes[d], last)[:, cols])
         nc.sync.dma_start(bias[:], b)
-
-        zeros = held.tile([P, picks], BF16, name="zeros")
-        nc.vector.memset(zeros[:], 0.0)
-        scratch = psum.tile([P, picks], F32, name="scratch")
-        for step in range(WARM_UP):
-            nc.tensor.matmul(scratch[:], zeros[:, :P], zeros[:], start=True, stop=True)
 
         layer_f32 = held.tile([P, blocks, features], F32, name="layer_f32")
         nc.scalar.copy(layer_f32[:], layer_bf16[:])
 
         def clamped_look_up(dst, k, d, cols):
-            first, last = d * picks + cols.start, d * picks + cols.stop
-            window = tables[k][:].indirect(offsets[:, first // GROUP : last // GROUP])
+            first, stop = d * picks + cols.start, d * picks + cols.stop
+            window = tables[k][:].indirect(offsets[:, first // GROUP : stop // GROUP])
             nc.vector.tensor_scalar(dst, window, LOW, HIGH, ALU.max, ALU.min)
 
-        acc = psum.tile([features, picks], F32, name="acc")
-        for k in range(blocks - 1):
+        acc_left = psum.tile([features, half], F32, name="acc_left")
+        acc_right = psum.tile([features, half], F32, name="acc_right")
+        result = held.tile([features, picks], F32, name="result")
+
+        def finish(acc, cols):
+            nc.scalar.activation(result[:, cols], acc[:], ACT.Relu, bias=bias[:])
+            nc.sync.dma_start(out[:, cols], result[:, cols])
+
+        for k in range(last):
             clamped = held.tile([P, depth, picks], F32, name=f"clamped{k}")
             products = held.tile([P, depth, picks], F32, name=f"products{k}")
             for d in range(depth):
-                clamped_look_up(clamped[:, d, :], k, d, slice(0, picks))
+                clamped_look_up(clamped[:, d, :], k, d, whole)
                 nc.gpsimd.tensor_tensor(products[:, d, :], clamped[:, d, :], weights[k][:, d, :], ALU.mult)
-                nc.tensor.matmul(acc[:], layer_f32[:, k, :], products[:, d, :], start=k == 0 and d == 0, stop=False)
+                for acc, cols in ((acc_left, left), (acc_right, right)):
+                    nc.tensor.matmul(acc[:], layer_f32[:, k, :], products[:, d, cols],
+                                     start=k == 0 and d == 0, stop=False)
 
-        k = blocks - 1
         clamped_left = held.tile([P, depth, half], F32, name="clamped_left")
         products_left = held.tile([P, depth, half], F32, name="products_left")
         for d in range(depth):
-            clamped_look_up(clamped_left[:, d, :], k, d, left)
-        nc.gpsimd.tensor_tensor(products_left[:], clamped_left[:], weights[k][:, :, left], ALU.mult)
+            clamped_look_up(clamped_left[:, d, :], last, d, left)
+        nc.gpsimd.tensor_tensor(products_left[:], clamped_left[:], weights_left[:], ALU.mult)
         for d in range(depth):
-            nc.tensor.matmul(acc[:, left], layer_f32[:, k, :], products_left[:, d, :], start=False, stop=False)
+            nc.tensor.matmul(acc_left[:], layer_f32[:, last, :], products_left[:, d, :],
+                             start=False, stop=d == depth - 1)
+        finish(acc_left, left)
 
         clamped_right = held.tile([P, depth, half], F32, name="clamped_right")
         products_right = held.tile([P, depth, half], F32, name="products_right")
         pair_sum = held.tile([P, half], F32, name="pair_sum")
         x_right = held.tile([P, half], BF16, name="x_right")
         for d in range(depth):
-            clamped_look_up(clamped_right[:, d, :], k, d, right)
-        nc.vector.tensor_tensor(products_right[:], clamped_right[:], weights[k][:, :, right], ALU.mult)
+            clamped_look_up(clamped_right[:, d, :], last, d, right)
+        nc.vector.tensor_tensor(products_right[:], clamped_right[:], weights_right[:], ALU.mult)
         nc.vector.tensor_tensor(pair_sum[:], products_right[:, 0, :], products_right[:, 1, :], ALU.add)
         nc.vector.tensor_tensor(x_right[:], pair_sum[:], products_right[:, 2, :], ALU.add)
-        nc.tensor.matmul(acc[:, right], layer_bf16[:, k, :], x_right[:], start=False, stop=True)
-
-        result = held.tile([features, picks], F32, name="result")
-        for cols in (left, right):
-            nc.scalar.activation(result[:, cols], acc[:, cols], ACT.Relu, bias=bias[:])
-            nc.sync.dma_start(out[:, cols], result[:, cols])
+        nc.tensor.matmul(acc_right[:], layer_bf16[:, last, :], x_right[:], start=False, stop=True)
+        finish(acc_right, right)

@@ -21,6 +21,7 @@ def tile_lookup_clipmix_relu_kernel(tc, tab, u0, u1, u2, w, b, offs, out):
     depth = len(mixes)
     half = picks // 2
     whole, left, right = slice(0, picks), slice(0, half), slice(half, picks)
+    first_two, third = slice(0, depth - 1), slice(depth - 1, depth)
 
     def block_rows(array, k):
         return array.rearrange("(p k) c -> k p c", k=blocks)[k]
@@ -62,10 +63,6 @@ def tile_lookup_clipmix_relu_kernel(tc, tab, u0, u1, u2, w, b, offs, out):
         acc_right = psum.tile([features, half], F32, name="acc_right")
         result = held.tile([features, picks], F32, name="result")
 
-        def finish(acc, cols):
-            nc.scalar.activation(result[:, cols], acc[:], ACT.Relu, bias=bias[:])
-            nc.sync.dma_start(out[:, cols], result[:, cols])
-
         for k in range(last):
             clamped = held.tile([P, depth, picks], F32, name=f"clamped{k}")
             products = held.tile([P, depth, picks], F32, name=f"products{k}")
@@ -80,11 +77,14 @@ def tile_lookup_clipmix_relu_kernel(tc, tab, u0, u1, u2, w, b, offs, out):
         products_left = held.tile([P, depth, half], F32, name="products_left")
         for d in range(depth):
             clamped_look_up(clamped_left[:, d, :], last, d, left)
-        nc.gpsimd.tensor_tensor(products_left[:], clamped_left[:], weights_left[:], ALU.mult)
+        for terms in (first_two, third):
+            nc.gpsimd.tensor_tensor(products_left[:, terms, :], clamped_left[:, terms, :], weights_left[:, terms, :],
+                                    ALU.mult)
         for d in range(depth):
             nc.tensor.matmul(acc_left[:], layer_f32[:, last, :], products_left[:, d, :],
                              start=False, stop=d == depth - 1)
-        finish(acc_left, left)
+        nc.scalar.activation(result[:, left], acc_left[:], ACT.Relu, bias=bias[:])
+        nc.sync.dma_start(out[:, left], result[:, left])
 
         clamped_right = held.tile([P, depth, half], F32, name="clamped_right")
         products_right = held.tile([P, depth, half], F32, name="products_right")
@@ -92,8 +92,11 @@ def tile_lookup_clipmix_relu_kernel(tc, tab, u0, u1, u2, w, b, offs, out):
         x_right = held.tile([P, half], BF16, name="x_right")
         for d in range(depth):
             clamped_look_up(clamped_right[:, d, :], last, d, right)
-        nc.vector.tensor_tensor(products_right[:], clamped_right[:], weights_right[:], ALU.mult)
+        for terms in (first_two, third):
+            nc.vector.tensor_tensor(products_right[:, terms, :], clamped_right[:, terms, :],
+                                    weights_right[:, terms, :], ALU.mult)
         nc.vector.tensor_tensor(pair_sum[:], products_right[:, 0, :], products_right[:, 1, :], ALU.add)
         nc.vector.tensor_tensor(x_right[:], pair_sum[:], products_right[:, 2, :], ALU.add)
         nc.tensor.matmul(acc_right[:], layer_bf16[:, last, :], x_right[:], start=False, stop=True)
-        finish(acc_right, right)
+        nc.vector.tensor_scalar(result[:, right], acc_right[:], bias[:], 0.0, ALU.add, ALU.max)
+        nc.sync.dma_start(out[:, right], result[:, right])

import concourse.mybir as mybir

F32, BF16, U16 = mybir.dt.float32, mybir.dt.bfloat16, mybir.dt.uint16
ALU = mybir.AluOpType
ACT = mybir.ActivationFunctionType

P = 128
GROUP = 16
LOW, HIGH = -1.25, 1.0
FLOPS = 2 * 512 * 128 * 512


def tile_lookup_clipmix_relu_kernel(tc, tab, u0, u1, u2, w, b, offs, out):
    nc = tc.nc
    rows, table_cols = tab.shape
    picks = u0.shape[1]
    features = w.shape[1]
    blocks = rows // P
    last = blocks - 1
    mixes = (u0, u1, u2)
    depth = len(mixes)
    half = picks // 2
    whole, left, right = slice(0, picks), slice(0, half), slice(half, picks)
    first_two, third = slice(0, depth - 1), slice(depth - 1, depth)

    def block_rows(array, k):
        return array.rearrange("(p k) c -> k p c", k=blocks)[k]

    with (
        tc.tile_pool(name="held", bufs=1) as held,
        tc.psum_pool(name="psum", bufs=1) as psum,
    ):
        offsets = held.tile(list(offs.shape), U16, name="offsets")
        tables = [held.tile([P, table_cols], F32, name=f"table{k}") for k in range(blocks)]
        weights = [held.tile([P, depth, picks], F32, name=f"weights{k}") for k in range(last)]
        weights_left = held.tile([P, depth, half], F32, name="weights_left")
        weights_right = held.tile([P, depth, half], F32, name="weights_right")
        layer_bf16 = held.tile([P, blocks, features], BF16, name="layer_bf16")
        bias = held.tile([features, 1], F32, name="bias")

        nc.sync.dma_start(tables[0][:], block_rows(tab, 0))
        nc.sync.dma_start(offsets[:], offs)
        nc.sync.dma_start(layer_bf16[:], w.rearrange("(p k) m -> p k m", k=blocks))
        for k in range(last):
            for d in range(depth):
                if d == depth - 1:
                    nc.sync.dma_start(tables[k + 1][:], block_rows(tab, k + 1))
                nc.sync.dma_start(weights[k][:, d, :], block_rows(mixes[d], k))
        for tile, cols in ((weights_left, left), (weights_right, right)):
            for d in range(depth):
                nc.sync.dma_start(tile[:, d, :], block_rows(mixes[d], last)[:, cols])
        nc.sync.dma_start(bias[:], b)

        layer_f32 = held.tile([P, blocks, features], F32, name="layer_f32")
        nc.scalar.copy(layer_f32[:], layer_bf16[:])

        def clamped_look_up(dst, k, d, cols):
            first, stop = d * picks + cols.start, d * picks + cols.stop
            window = tables[k][:].indirect(offsets[:, first // GROUP : stop // GROUP])
            nc.vector.tensor_scalar(dst, window, LOW, HIGH, ALU.max, ALU.min)

        acc_left = psum.tile([features, half], F32, name="acc_left")
        acc_right = psum.tile([features, half], F32, name="acc_right")
        result = held.tile([features, picks], F32, name="result")

        for k in range(last):
            clamped = held.tile([P, depth, picks], F32, name=f"clamped{k}")
            products = held.tile([P, depth, picks], F32, name=f"products{k}")
            for d in range(depth):
                clamped_look_up(clamped[:, d, :], k, d, whole)
                nc.gpsimd.tensor_tensor(products[:, d, :], clamped[:, d, :], weights[k][:, d, :], ALU.mult)
                for acc, cols in ((acc_left, left), (acc_right, right)):
                    nc.tensor.matmul(acc[:], layer_f32[:, k, :], products[:, d, cols],
                                     start=k == 0 and d == 0, stop=False)

        clamped_left = held.tile([P, depth, half], F32, name="clamped_left")
        products_left = held.tile([P, depth, half], F32, name="products_left")
        for d in range(depth):
            clamped_look_up(clamped_left[:, d, :], last, d, left)
        for terms in (first_two, third):
            nc.gpsimd.tensor_tensor(products_left[:, terms, :], clamped_left[:, terms, :], weights_left[:, terms, :],
                                    ALU.mult)
        for d in range(depth):
            nc.tensor.matmul(acc_left[:], layer_f32[:, last, :], products_left[:, d, :],
                             start=False, stop=d == depth - 1)
        nc.scalar.activation(result[:, left], acc_left[:], ACT.Relu, bias=bias[:])
        nc.sync.dma_start(out[:, left], result[:, left])

        clamped_right = held.tile([P, depth, half], F32, name="clamped_right")
        products_right = held.tile([P, depth, half], F32, name="products_right")
        pair_sum = held.tile([P, half], F32, name="pair_sum")
        x_right = held.tile([P, half], BF16, name="x_right")
        for d in range(depth):
            clamped_look_up(clamped_right[:, d, :], last, d, right)
        for terms in (first_two, third):
            nc.vector.tensor_tensor(products_right[:, terms, :], clamped_right[:, terms, :],
                                    weights_right[:, terms, :], ALU.mult)
        nc.vector.tensor_tensor(pair_sum[:], products_right[:, 0, :], products_right[:, 1, :], ALU.add)
        nc.vector.tensor_tensor(x_right[:], pair_sum[:], products_right[:, 2, :], ALU.add)
        nc.tensor.matmul(acc_right[:], layer_bf16[:, last, :], x_right[:], start=False, stop=True)
        nc.vector.tensor_scalar(result[:, right], acc_right[:], bias[:], 0.0, ALU.add, ALU.max)
        nc.sync.dma_start(out[:, right], result[:, right])
